import numpy as np
import ml_dtypes


def mxq(x, axis, fmt="e4m3"):
    dtype, down = {"e4m3": (ml_dtypes.float8_e4m3fn, 7), "e5m2": (ml_dtypes.float8_e5m2, 14)}[fmt]
    v = np.moveaxis(np.asarray(x, np.float32).astype(ml_dtypes.bfloat16).astype(np.float64), axis, -1)
    blocks = v.reshape(v.shape[:-1] + (-1, 32))
    amax = np.abs(blocks).max(-1, keepdims=True)
    byte = np.maximum(np.where(amax > 0, np.frexp(amax)[1] - 1 + 127, 0) - down, 1)
    scale = np.exp2(byte - 127.0)
    codes = (blocks / scale).astype(np.float32).astype(dtype).astype(np.float64)
    return np.moveaxis((codes * scale).reshape(v.shape), -1, axis)


WIDE = False


def mx_kscale(k):
    if not WIDE:
        return np.ones(k)
    levels = np.array([10, -10, 5, -5, 0])
    if k % 512:
        return np.exp2(np.random.permutation(np.resize(levels, k // 32))).repeat(32)
    a = np.empty((k // 512, 16))
    for p in range(k // 512):
        a[p, :8] = np.random.permutation(np.resize(levels, 8))
        for g in range(8):
            far = levels[np.abs(levels - a[p, g]) >= 10]
            a[p, g + 8] = far[np.random.randint(len(far))]
    return np.exp2(a.ravel()).repeat(32)


def f64(x):
    return np.asarray(x).astype(np.float64)


def striped(idx):
    return np.tile(idx.reshape(-1, 16).T, (8, 1)).astype(np.uint16)


def unstriped(offs):
    return offs[:16].T.reshape(-1).astype(np.int64)


E2M1 = np.array([0.0, 0.5, 1.0, 1.5, 2.0, 3.0, 4.0, 6.0, -0.0, -0.5, -1.0, -1.5, -2.0, -3.0, -4.0, -6.0])


def pack_weight(w, fmt):
    k, n = w.shape
    w = f64(np.asarray(w, np.float32).astype(ml_dtypes.bfloat16)).reshape(k // 32, 32, n)
    amax = np.abs(w).max(1)
    if fmt == "e4m3":
        byte = np.frexp(amax)[1] - 1 + 127 - 7
    else:
        mant, ex = np.frexp(amax / 6.0)
        byte = np.where(mant > 0.5, ex, ex - 1) + 127
    byte = np.clip(np.where(amax > 0, byte, 1), 1, 254)
    scaled = (w * np.exp2(127.0 - byte)[:, None, :]).reshape(k, n).astype(np.float32)
    by_word = np.ascontiguousarray(scaled.reshape(k // 512, 128, 4, n).transpose(0, 1, 3, 2))
    if fmt == "e4m3":
        words = by_word.astype(ml_dtypes.float8_e4m3fn).view(np.uint8)
    else:
        c = by_word.astype(ml_dtypes.float4_e2m1fn).view(np.uint8) & 0xF
        words = (c[..., 0::2] | (c[..., 1::2] << 4)).reshape(k // 512, 128, 2 * n)
    return np.ascontiguousarray(words), np.ascontiguousarray(byte.astype(np.uint8).reshape(k // 512, 16, n))


def unpack_weight(words, scales, fmt):
    g, _, n = scales.shape
    words = np.ascontiguousarray(words).reshape(g, 128, n, -1)
    if fmt == "e4m3":
        vals = words.view(ml_dtypes.float8_e4m3fn).astype(np.float64)
    else:
        nib = np.empty((g, 128, n, 4), np.uint8)
        nib[..., 0::2] = words & 0xF
        nib[..., 1::2] = words >> 4
        vals = E2M1[nib]
    vals = vals * np.repeat(np.exp2(scales.astype(np.float64) - 127.0), 8, axis=1)[..., None]
    return vals.transpose(0, 1, 3, 2).reshape(g * 512, n)


def relu(v):
    return np.maximum(v, 0.0)


K, T, E, H, N = 1024, 768, 6, 512, 128
COUNTS = (128, 128, 128, 256, 384, 512)
STARTS = np.cumsum((0,) + COUNTS)


def by_expert(wq, xq):
    return np.concatenate([wq[e].T @ xq[:, STARTS[e]:STARTS[e + 1]] for e in range(E)], axis=1)


def setup_inputs():
    n = np.random.standard_normal
    s = mx_kscale(K)[:, None]
    u = mx_kscale(H)
    both = np.repeat(np.arange(E), COUNTS)
    pair = np.stack([both[:T], both[T:]])[:, np.random.permutation(T)]
    pair = np.where(np.random.rand(T) < 0.5, pair, pair[::-1])
    order = np.argsort(pair.reshape(-1), kind="stable")
    slot_token = order % T; pos = np.empty(2 * T, np.int64); pos[order] = np.arange(2 * T); pos = pos.reshape(2, T)
    g = np.random.uniform(0.2, 0.8, T)
    w1 = [pack_weight(m, "e2m1") for m in n((E, K, H)) / np.sqrt(K) / s[None] * u[None, None, :]]
    w2 = [pack_weight(m, "e2m1") for m in n((E, H, N)) / np.sqrt(H) / u[None, :, None]]
    return {
        "xT": (n((K, T)) * s).astype(np.float32),
        "w1_words": np.stack([m[0] for m in w1]),
        "w1_scales": np.stack([m[1] for m in w1]),
        "w2_words": np.stack([m[0] for m in w2]),
        "w2_scales": np.stack([m[1] for m in w2]),
        "gate": np.stack([np.tile(g, (N, 1)), np.tile(1.0 - g, (N, 1))]).astype(np.float32),
        "offs": striped(slot_token),
        "pos1": striped(pos[0]),
        "pos2": striped(pos[1]),
    }


def reference(xT, w1_words, w1_scales, w2_words, w2_scales, gate, offs, pos1, pos2):
    idx = unstriped(offs)
    w1 = np.stack([unpack_weight(w1_words[e], w1_scales[e], "e2m1") for e in range(E)])
    w2 = np.stack([unpack_weight(w2_words[e], w2_scales[e], "e2m1") for e in range(E)])
    xq = mxq(f64(xT)[:, idx], 0, "e4m3")
    h = relu(by_expert(w1, xq))
    y = by_expert(w2, mxq(h, 0, "e4m3"))
    return f64(gate[0]) * y[:, unstriped(pos1)] + f64(gate[1]) * y[:, unstriped(pos2)]

@@ -1,0 +1,300 @@
+from contextlib import ExitStack
+
+import concourse.mybir as mybir
+from concourse.masks import make_identity
+
+K, T, E, H, N = 1024, 768, 6, 512, 128
+COUNTS = (128, 128, 128, 256, 384, 512)
+S = sum(COUNTS)
+FLOPS = 2 * S * (K * H + H * N)
+
+F32 = mybir.dt.float32
+BF16 = mybir.dt.bfloat16
+U32 = mybir.dt.uint32
+I32 = mybir.dt.int32
+U16 = mybir.dt.uint16
+U8 = mybir.dt.uint8
+FP8X4 = mybir.dt.float8_e4m3fn_x4
+FP4X4 = mybir.dt.float4_e2m1fn_x4
+RELU = mybir.ActivationFunctionType.Relu
+MULT = mybir.AluOpType.mult
+ADD = mybir.AluOpType.add
+MAX = mybir.AluOpType.max
+
+P = 128
+TC = 256
+VSHARE = 160
+EXPERT_OF_TILE = [e for e in range(E) for c in range(COUNTS[e] // P)]
+
+
+def tile_moe_rag_mlp_relu_kernel(
+    tc, xT, w1_words, w1_scales, w2_words, w2_scales, gate, offs, pos1, pos2, out
+):
+    nc = tc.nc
+    with ExitStack() as ctx:
+        lists = ctx.enter_context(tc.tile_pool(name="lists", bufs=1))
+        keep = ctx.enter_context(tc.tile_pool(name="keep", bufs=1))
+        work = ctx.enter_context(tc.tile_pool(name="work", bufs=3))
+        psum_a = ctx.enter_context(tc.psum_pool(name="psum_a", bufs=4))
+        psum_t = ctx.enter_context(tc.psum_pool(name="psum_t", bufs=2))
+        psum_y = ctx.enter_context(tc.psum_pool(name="psum_y", bufs=2))
+
+        offs_sb = lists.tile([P, S // 16], U16, name="offs_sb")
+        pos1_sb = lists.tile([P, T // 16], U16, name="pos1_sb")
+        pos2_sb = lists.tile([P, T // 16], U16, name="pos2_sb")
+
+        x_scales = []
+        for s in range(2):
+            t = keep.tile([P, T], U8, name=f"x_scales{s}", align_bytes=64)
+            x_scales.append(t)
+        w1_sc = keep.tile([P, 2 * E, H], U8, name="w1_sc", align_bytes=64)
+        w2_sc = keep.tile([P, E, N], U8, name="w2_sc", align_bytes=64)
+        ident = keep.tile([P, P], F32, name="ident", align_bytes=64)
+        nc.vector.memset(w1_sc[:].rearrange("p a b -> p (a b)").bitcast(I32), 0)
+        nc.gpsimd.memset(x_scales[0][:], 0)
+        nc.vector.memset(w2_sc[:].rearrange("p a b -> p (a b)").bitcast(I32), 0)
+        nc.gpsimd.memset(x_scales[1][:], 0)
+        make_identity(nc, ident[:])
+
+        xv = xT.rearrange("(s p j) t -> s p j t", s=2, j=4)
+        raw = {}
+
+        def load_x(s):
+            for c in range(T // TC):
+                r = keep.tile([P, 4, TC], F32, name=f"x_raw{s}_{c}")
+                nc.sync.dma_start(out=r[:], in_=xv[s][:, :, c * TC : (c + 1) * TC])
+                raw[s, c] = r
+
+        w1_sb = {}
+
+        def load_w1(e):
+            w = keep.tile([P, 2, 2 * H], U8, name=f"w1_sb{e}", align_bytes=64)
+            nc.sync.dma_start(
+                out=w[:].bitcast(I32), in_=w1_words[e].rearrange("s p n -> p s n").bitcast(I32)
+            )
+            w1_sb[e] = w
+
+        load_x(0)
+        nc.sync.dma_start(out=offs_sb[:], in_=offs)
+        w1_sv = w1_scales.rearrange("e s (q r) i -> r q (e s) i", r=4)
+        for r in range(4):
+            nc.sync.dma_start(out=w1_sc[r:P:32].bitcast(I32), in_=w1_sv[r].bitcast(I32))
+        load_w1(5)
+        load_x(1)
+        load_w1(4)
+        load_w1(3)
+        w2_sb = keep.tile([P, E, 2 * N], U8, name="w2_sb", align_bytes=64)
+        nc.sync.dma_start(
+            out=w2_sb[:].bitcast(I32), in_=w2_words.rearrange("e s p n -> p (e s) n").bitcast(I32)
+        )
+        w2_sv = w2_scales.rearrange("e s (q r) i -> r q (e s) i", r=4)
+        for r in range(4):
+            nc.sync.dma_start(out=w2_sc[r:P:32].bitcast(I32), in_=w2_sv[r].bitcast(I32))
+        for e in (2, 1, 0):
+            load_w1(e)
+        gates = []
+        for c in range(2):
+            g = keep.tile([P, T], F32, name=f"gate{c}")
+            gates.append(g)
+            nc.sync.dma_start(out=g[:], in_=gate[c])
+        nc.sync.dma_start(out=pos1_sb[:], in_=pos1)
+        nc.sync.dma_start(out=pos2_sb[:], in_=pos2)
+
+        x_codes = []
+        for s in range(2):
+            t = keep.tile([P, T], U32, name=f"x_codes{s}", align_bytes=64)
+            x_codes.append(t)
+        grouped = {}
+
+        def cast_x(s, c, vshare):
+            g = keep.tile([P, TC, 4], BF16, name=f"x_grouped{s}_{c}", align_bytes=64)
+            src = raw[s, c][:].rearrange("p j t -> p t j")
+            if vshare:
+                nc.vector.tensor_copy(out=g[:, :vshare], in_=src[:, :vshare])
+            if vshare < TC:
+                nc.scalar.copy(out=g[:, vshare:], in_=src[:, vshare:])
+            grouped[s, c] = g
+
+        def quantise_x(s, c):
+            cols = slice(c * TC, (c + 1) * TC)
+            nc.vector.quantize_mx(
+                out=x_codes[s][:, cols].bitcast(FP8X4),
+                scales=x_scales[s][:, cols],
+                in_=grouped[s, c][:].rearrange("p t j -> p (t j)"),
+            )
+
+        slot_codes, slot_scales = {}, {}
+
+        def gather(s, t0, t1, what):
+            n = (t1 - t0) * P
+            ofs = offs_sb[:, t0 * P // 16 : t1 * P // 16]
+            if what == "w":
+                g = keep.tile([P, n], U32, name=f"slot_codes{s}_{t0}", align_bytes=64)
+                nc.vector.tensor_copy(out=g[:], in_=x_codes[s][:].indirect(ofs))
+                dst = slot_codes
+            else:
+                g = keep.tile([P, n], U8, name=f"slot_scales{s}_{t0}", align_bytes=64)
+                nc.vector.tensor_copy(out=g[:], in_=x_scales[s][:].indirect(ofs))
+                dst = slot_scales
+            for t in range(t0, t1):
+                dst[s, t] = (g, (t - t0) * P)
+
+        acc = {}
+
+        def mm1(t, s):
+            e = EXPERT_OF_TILE[t]
+            if s == 0:
+                a = psum_a.tile([P, H], F32, name="acc")
+                acc[t] = a
+            g, c0 = slot_codes[s, t]
+            z, z0 = slot_scales[s, t]
+            nc.tensor.matmul_mx(
+                out=acc[t][:],
+                lhsT=g[:, c0 : c0 + P].bitcast(FP8X4),
+                lhsT_scale=z[:, z0 : z0 + P],
+                rhs=w1_sb[e][:, s].bitcast(FP4X4),
+                rhs_scale=w1_sc[:, 2 * e + s],
+                start=(s == 0),
+                stop=(s == 1),
+            )
+
+        hid = {}
+
+        def relu(t, engine):
+            h = work.tile([P, 2, P, 2], BF16, name="hid", align_bytes=64)
+            src = acc[t][:].rearrange("p (r u e) -> p u r e", u=2, e=2)
+            if engine == "v":
+                nc.vector.tensor_scalar(out=h[:], in0=src, scalar1=0.0, scalar2=None, op0=MAX)
+            else:
+                nc.scalar.activation(out=h[:], in_=src, func=RELU)
+            hid[t] = h
+
+        turned = {}
+
+        def turn(t0, n):
+            x = psum_t.tile([P, 2, 2, P], F32, name="turned")
+            for j in range(n):
+                words = hid[t0 + j][:].rearrange("p u r e -> p (u r e)").bitcast(F32)
+                for u in range(2):
+                    nc.tensor.transpose(x[:, j, u], words[:, u * P : (u + 1) * P], ident[:])
+            turned[t0] = x
+
+        h_grouped = {}
+
+        def ungroup(t0, n, engine):
+            g = work.tile([P, 2 * P, 4], BF16, name="h_grouped", align_bytes=64)
+            dst = g[:, : n * P].rearrange("p n i -> p (n i)").bitcast(F32).rearrange("p (j n u) -> p j n u", j=n, u=2)
+            src = turned[t0][:, :n].rearrange("p j u n -> p j n u")
+            if engine == "v":
+                nc.vector.tensor_copy(out=dst, in_=src)
+            else:
+                nc.scalar.copy(out=dst, in_=src)
+            h_grouped[t0] = g
+
+        hq = {}
+
+        def quantise_h(t0, n):
+            c = work.tile([P, 2 * P], U32, name="h_codes", align_bytes=64)
+            z = work.tile([P, 2 * P], U8, name="h_scales", align_bytes=64)
+            nc.vector.quantize_mx(
+                out=c[:, : n * P].bitcast(FP8X4), scales=z[:, : n * P],
+                in_=h_grouped[t0][:, : n * P].rearrange("p n i -> p (n i)"),
+            )
+            hq[t0] = (c, z)
+
+        y_all = keep.tile([P, S], F32, name="y_all", align_bytes=64)
+
+        def layer2(t0, n, engine):
+            c, z = hq[t0]
+            y = psum_y.tile([P, 2 * P], F32, name="y")
+            if n == 1:
+                spans = [(t0, 0, P)]
+            elif EXPERT_OF_TILE[t0] == EXPERT_OF_TILE[t0 + 1]:
+                spans = [(t0, 0, 2 * P)]
+            else:
+                spans = [(t0, 0, P), (t0 + 1, P, P)]
+            for t, c0, w in spans:
+                e = EXPERT_OF_TILE[t]
+                nc.tensor.matmul_mx(
+                    out=y[:, c0 : c0 + w],
+                    lhsT=w2_sb[:, e].bitcast(FP4X4),
+                    lhsT_scale=w2_sc[:, e],
+                    rhs=c[:, c0 : c0 + w].bitcast(FP8X4),
+                    rhs_scale=z[:, c0 : c0 + w],
+                    start=True,
+                    stop=True,
+                )
+            dst = y_all[:, t0 * P : (t0 + n) * P]
+            if engine == "v":
+                nc.vector.tensor_copy(out=dst, in_=y[:, : n * P])
+            else:
+                nc.scalar.copy(out=dst, in_=y[:, : n * P])
+
+        for c in range(3):
+            cast_x(0, c, VSHARE)
+            quantise_x(0, c)
+        for c in range(3):
+            cast_x(1, c, 0)
+
+        def mm(t):
+            mm1(t, 0)
+            mm1(t, 1)
+
+        def chain(t0, n, relu_engines="ss", copy_engine="s", y_engine="s"):
+            for j in range(n):
+                relu(t0 + j, relu_engines[j])
+            turn(t0, n)
+            ungroup(t0, n, copy_engine)
+            quantise_h(t0, n)
+            layer2(t0, n, y_engine)
+
+        gather(0, 8, 12, "w")
+        gather(0, 8, 12, "b")
+        for t in range(8, 12):
+            mm1(t, 0)
+        gather(0, 4, 8, "w")
+        gather(0, 4, 8, "b")
+        for c in range(3):
+            quantise_x(1, c)
+        for t in (8, 10):
+            gather(1, t, t + 2, "w")
+            gather(1, t, t + 2, "b")
+            mm1(t, 1)
+            mm1(t + 1, 1)
+        chain(8, 2)
+        gather(1, 6, 8, "w")
+        gather(1, 6, 8, "b")
+        mm(6)
+        mm(7)
+        chain(10, 2)
+        gather(1, 4, 6, "w")
+        gather(1, 4, 6, "b")
+        mm(4)
+        mm(5)
+        chain(6, 2)
+        gather(0, 0, 4, "w")
+        gather(0, 0, 4, "b")
+        chain(4, 2)
+        gather(1, 2, 4, "w")
+        gather(1, 2, 4, "b")
+        mm(2)
+        mm(3)
+        gather(1, 0, 2, "w")
+        gather(1, 1, 2, "b")
+        mm(1)
+        gather(1, 0, 1, "b")
+        mm(0)
+        chain(2, 2)
+        chain(1, 1)
+        chain(0, 1, "v", "v", "v")
+
+        halves = ((0, 384), (384, 768))
+        for a, b in halves:
+            cols = slice(a // 16, b // 16)
+            o1 = keep.tile([P, b - a], F32, name=f"first{a}")
+            o2 = keep.tile([P, b - a], F32, name=f"second{a}")
+            nc.vector.tensor_tensor(out=o1[:], in0=y_all[:].indirect(pos1_sb[:, cols]), in1=gates[0][:, a:b], op=MULT)
+            nc.vector.tensor_tensor(out=o2[:], in0=y_all[:].indirect(pos2_sb[:, cols]), in1=gates[1][:, a:b], op=MULT)
+            o = keep.tile([P, b - a], F32, name=f"result{a}")
+            nc.vector.tensor_tensor(out=o[:], in0=o1[:], in1=o2[:], op=ADD)
+            nc.sync.dma_start(out=out[:, a:b], in_=o[:])

@@ -76,11 +76,11 @@ def tile_moe_rag_mlp_relu_kernel(
 
         load_x(0)
         nc.sync.dma_start(out=offs_sb[:], in_=offs)
+        load_x(1)
         w1_sv = w1_scales.rearrange("e s (q r) i -> r q (e s) i", r=4)
         for r in range(4):
             nc.sync.dma_start(out=w1_sc[r:P:32].bitcast(I32), in_=w1_sv[r].bitcast(I32))
         load_w1(5)
-        load_x(1)
         load_w1(4)
         load_w1(3)
         w2_sb = keep.tile([P, E, 2 * N], U8, name="w2_sb", align_bytes=64)
@@ -230,30 +230,33 @@ def tile_moe_rag_mlp_relu_kernel(
             else:
                 nc.scalar.copy(out=dst, in_=y[:, : n * P])
 
+        VS0 = 208
         for c in range(3):
-            cast_x(0, c, VSHARE)
+            cast_x(0, c, VS0)
             quantise_x(0, c)
         for c in range(3):
-            cast_x(1, c, 0)
+            cast_x(1, c, (64, 64, 160)[c])
 
         def mm(t):
             mm1(t, 0)
             mm1(t, 1)
 
-        def chain(t0, n, relu_engines="ss", copy_engine="s", y_engine="s"):
+        RELUS = "sssvssssssss"
+        UNGROUPS = {0: "v", 1: "s", 2: "v", 4: "v", 6: "s", 8: "s", 10: "s"}
+        YCOPIES = {0: "v", 1: "s", 2: "s", 4: "s", 6: "s", 8: "s", 10: "s"}
+
+        def chain(t0, n):
             for j in range(n):
-                relu(t0 + j, relu_engines[j])
+                relu(t0 + j, RELUS[t0 + j])
             turn(t0, n)
-            ungroup(t0, n, copy_engine)
+            ungroup(t0, n, UNGROUPS[t0])
             quantise_h(t0, n)
-            layer2(t0, n, y_engine)
+            layer2(t0, n, YCOPIES[t0])
 
         gather(0, 8, 12, "w")
         gather(0, 8, 12, "b")
         for t in range(8, 12):
             mm1(t, 0)
-        gather(0, 4, 8, "w")
-        gather(0, 4, 8, "b")
         for c in range(3):
             quantise_x(1, c)
         for t in (8, 10):
@@ -261,6 +264,8 @@ def tile_moe_rag_mlp_relu_kernel(
             gather(1, t, t + 2, "b")
             mm1(t, 1)
             mm1(t + 1, 1)
+        gather(0, 4, 8, "w")
+        gather(0, 4, 8, "b")
         chain(8, 2)
         gather(1, 6, 8, "w")
         gather(1, 6, 8, "b")
@@ -286,9 +291,9 @@ def tile_moe_rag_mlp_relu_kernel(
         mm(0)
         chain(2, 2)
         chain(1, 1)
-        chain(0, 1, "v", "v", "v")
+        chain(0, 1)
 
-        halves = ((0, 384), (384, 768))
+        halves = ((0, 512), (512, 768))
         for a, b in halves:
             cols = slice(a // 16, b // 16)
             o1 = keep.tile([P, b - a], F32, name=f"first{a}")

@@ -35,6 +35,7 @@ def tile_moe_rag_mlp_relu_kernel(
         lists = ctx.enter_context(tc.tile_pool(name="lists", bufs=1))
         keep = ctx.enter_context(tc.tile_pool(name="keep", bufs=1))
         work = ctx.enter_context(tc.tile_pool(name="work", bufs=3))
+        late = ctx.enter_context(tc.tile_pool(name="late", bufs=3))
         psum_a = ctx.enter_context(tc.psum_pool(name="psum_a", bufs=4))
         psum_t = ctx.enter_context(tc.psum_pool(name="psum_t", bufs=2))
         psum_y = ctx.enter_context(tc.psum_pool(name="psum_y", bufs=2))
@@ -76,11 +77,18 @@ def tile_moe_rag_mlp_relu_kernel(
 
         load_x(0)
         nc.sync.dma_start(out=offs_sb[:], in_=offs)
-        load_x(1)
         w1_sv = w1_scales.rearrange("e s (q r) i -> r q (e s) i", r=4)
-        for r in range(4):
-            nc.sync.dma_start(out=w1_sc[r:P:32].bitcast(I32), in_=w1_sv[r].bitcast(I32))
+
+        def load_w1_scales(a, b):
+            for r in range(4):
+                nc.sync.dma_start(
+                    out=w1_sc[r:P:32, 2 * a : 2 * b].bitcast(I32), in_=w1_sv[r][:, 2 * a : 2 * b].bitcast(I32)
+                )
+
+        load_w1_scales(5, 6)
+        load_x(1)
         load_w1(5)
+        load_w1_scales(0, 5)
         load_w1(4)
         load_w1(3)
         w2_sb = keep.tile([P, E, 2 * N], U8, name="w2_sb", align_bytes=64)
@@ -107,12 +115,17 @@ def tile_moe_rag_mlp_relu_kernel(
         grouped = {}
 
         def cast_x(s, c, vshare):
-            g = keep.tile([P, TC, 4], BF16, name=f"x_grouped{s}_{c}", align_bytes=64)
-            src = raw[s, c][:].rearrange("p j t -> p t j")
-            if vshare:
-                nc.vector.tensor_copy(out=g[:, :vshare], in_=src[:, :vshare])
+            if s == 0:
+                g = keep.tile([P, TC, 4], BF16, name=f"x_grouped{s}_{c}", align_bytes=64)
+            else:
+                g = late.tile([P, TC, 4], BF16, name=f"x_grouped{s}_{c}", tag="late", align_bytes=64)
+            src = raw[s, c][:].rearrange("p j (c i) -> p c j i", i=4)
+            dst = g[:].rearrange("p (c i) j -> p c j i", i=4)
+            v = vshare // 4
+            if v:
+                nc.vector.tensor_copy(out=dst[:, :v], in_=src[:, :v])
             if vshare < TC:
-                nc.scalar.copy(out=g[:, vshare:], in_=src[:, vshare:])
+                nc.scalar.copy(out=dst[:, v:], in_=src[:, v:])
             grouped[s, c] = g
 
         def quantise_x(s, c):
@@ -128,12 +141,13 @@ def tile_moe_rag_mlp_relu_kernel(
         def gather(s, t0, t1, what):
             n = (t1 - t0) * P
             ofs = offs_sb[:, t0 * P // 16 : t1 * P // 16]
+            pool, tag = (late, "late") if s == 0 and t0 < 8 else (keep, f"slot_{what}{s}_{t0}")
             if what == "w":
-                g = keep.tile([P, n], U32, name=f"slot_codes{s}_{t0}", align_bytes=64)
+                g = pool.tile([P, n], U32, name=f"slot_codes{s}_{t0}", tag=tag, align_bytes=64)
                 nc.vector.tensor_copy(out=g[:], in_=x_codes[s][:].indirect(ofs))
                 dst = slot_codes
             else:
-                g = keep.tile([P, n], U8, name=f"slot_scales{s}_{t0}", align_bytes=64)
+                g = pool.tile([P, n], U8, name=f"slot_scales{s}_{t0}", tag=tag, align_bytes=64)
                 nc.vector.tensor_copy(out=g[:], in_=x_scales[s][:].indirect(ofs))
                 dst = slot_scales
             for t in range(t0, t1):
@@ -230,19 +244,19 @@ def tile_moe_rag_mlp_relu_kernel(
             else:
                 nc.scalar.copy(out=dst, in_=y[:, : n * P])
 
-        VS0 = 208
+        VS0 = 160
         for c in range(3):
             cast_x(0, c, VS0)
             quantise_x(0, c)
         for c in range(3):
-            cast_x(1, c, (64, 64, 160)[c])
+            cast_x(1, c, (64, 0, 160)[c])
 
         def mm(t):
             mm1(t, 0)
             mm1(t, 1)
 
         RELUS = "sssvssssssss"
-        UNGROUPS = {0: "v", 1: "s", 2: "v", 4: "v", 6: "s", 8: "s", 10: "s"}
+        UNGROUPS = {0: "s", 1: "s", 2: "v", 4: "s", 6: "s", 8: "s", 10: "s"}
         YCOPIES = {0: "v", 1: "s", 2: "s", 4: "s", 6: "s", 8: "s", 10: "s"}
 
         def chain(t0, n):
@@ -259,11 +273,11 @@ def tile_moe_rag_mlp_relu_kernel(
             mm1(t, 0)
         for c in range(3):
             quantise_x(1, c)
-        for t in (8, 10):
-            gather(1, t, t + 2, "w")
-            gather(1, t, t + 2, "b")
-            mm1(t, 1)
-            mm1(t + 1, 1)
+        for t0, t1 in ((8, 9), (9, 12)):
+            gather(1, t0, t1, "w")
+            gather(1, t0, t1, "b")
+            for t in range(t0, t1):
+                mm1(t, 1)
         gather(0, 4, 8, "w")
         gather(0, 4, 8, "b")
         chain(8, 2)

@@ -61,10 +61,11 @@ def tile_moe_rag_mlp_relu_kernel(
         raw = {}
 
         def load_x(s):
-            for c in range(T // TC):
-                r = keep.tile([P, 4, TC], F32, name=f"x_raw{s}_{c}")
-                nc.sync.dma_start(out=r[:], in_=xv[s][:, :, c * TC : (c + 1) * TC])
-                raw[s, c] = r
+            for a, b in ((0, 2), (2, 3)):
+                r = keep.tile([P, 4, (b - a) * TC], F32, name=f"x_raw{s}_{a}")
+                nc.sync.dma_start(out=r[:], in_=xv[s][:, :, a * TC : b * TC])
+                for c in range(a, b):
+                    raw[s, c] = (r, (c - a) * TC)
 
         w1_sb = {}
 
@@ -119,7 +120,8 @@ def tile_moe_rag_mlp_relu_kernel(
                 g = keep.tile([P, TC, 4], BF16, name=f"x_grouped{s}_{c}", align_bytes=64)
             else:
                 g = late.tile([P, TC, 4], BF16, name=f"x_grouped{s}_{c}", tag="late", align_bytes=64)
-            src = raw[s, c][:].rearrange("p j (c i) -> p c j i", i=4)
+            r, t0 = raw[s, c]
+            src = r[:, :, t0 : t0 + TC].rearrange("p j (c i) -> p c j i", i=4)
             dst = g[:].rearrange("p (c i) j -> p c j i", i=4)
             v = vshare // 4
             if v:
@@ -244,20 +246,20 @@ def tile_moe_rag_mlp_relu_kernel(
             else:
                 nc.scalar.copy(out=dst, in_=y[:, : n * P])
 
-        VS0 = 160
+        VS0 = (192, 64, 144)
         for c in range(3):
-            cast_x(0, c, VS0)
+            cast_x(0, c, VS0[c])
             quantise_x(0, c)
         for c in range(3):
-            cast_x(1, c, (64, 0, 160)[c])
+            cast_x(1, c, (96, 128, 160)[c])
 
         def mm(t):
             mm1(t, 0)
             mm1(t, 1)
 
-        RELUS = "sssvssssssss"
-        UNGROUPS = {0: "s", 1: "s", 2: "v", 4: "s", 6: "s", 8: "s", 10: "s"}
-        YCOPIES = {0: "v", 1: "s", 2: "s", 4: "s", 6: "s", 8: "s", 10: "s"}
+        RELUS = "vsssssssssss"
+        UNGROUPS = {0: "s", 1: "s", 2: "s", 4: "v", 6: "s", 8: "s", 10: "s"}
+        YCOPIES = {0: "v", 1: "s", 2: "s", 4: "v", 6: "v", 8: "s", 10: "s"}
 
         def chain(t0, n):
             for j in range(n):
@@ -273,7 +275,7 @@ def tile_moe_rag_mlp_relu_kernel(
             mm1(t, 0)
         for c in range(3):
             quantise_x(1, c)
-        for t0, t1 in ((8, 9), (9, 12)):
+        for t0, t1 in ((8, 10), (10, 12)):
             gather(1, t0, t1, "w")
             gather(1, t0, t1, "b")
             for t in range(t0, t1):

from contextlib import ExitStack

import concourse.mybir as mybir
from concourse.masks import make_identity

K, T, E, H, N = 1024, 768, 6, 512, 128
COUNTS = (128, 128, 128, 256, 384, 512)
S = sum(COUNTS)
FLOPS = 2 * S * (K * H + H * N)

F32 = mybir.dt.float32
BF16 = mybir.dt.bfloat16
U32 = mybir.dt.uint32
I32 = mybir.dt.int32
U16 = mybir.dt.uint16
U8 = mybir.dt.uint8
FP8X4 = mybir.dt.float8_e4m3fn_x4
FP4X4 = mybir.dt.float4_e2m1fn_x4
RELU = mybir.ActivationFunctionType.Relu
MULT = mybir.AluOpType.mult
ADD = mybir.AluOpType.add
MAX = mybir.AluOpType.max

P = 128
TC = 256
VSHARE = 160
EXPERT_OF_TILE = [e for e in range(E) for c in range(COUNTS[e] // P)]


def tile_moe_rag_mlp_relu_kernel(
    tc, xT, w1_words, w1_scales, w2_words, w2_scales, gate, offs, pos1, pos2, out
):
    nc = tc.nc
    with ExitStack() as ctx:
        lists = ctx.enter_context(tc.tile_pool(name="lists", bufs=1))
        keep = ctx.enter_context(tc.tile_pool(name="keep", bufs=1))
        work = ctx.enter_context(tc.tile_pool(name="work", bufs=3))
        late = ctx.enter_context(tc.tile_pool(name="late", bufs=3))
        psum_a = ctx.enter_context(tc.psum_pool(name="psum_a", bufs=4))
        psum_t = ctx.enter_context(tc.psum_pool(name="psum_t", bufs=2))
        psum_y = ctx.enter_context(tc.psum_pool(name="psum_y", bufs=2))

        offs_sb = lists.tile([P, S // 16], U16, name="offs_sb")
        pos1_sb = lists.tile([P, T // 16], U16, name="pos1_sb")
        pos2_sb = lists.tile([P, T // 16], U16, name="pos2_sb")

        x_scales = []
        for s in range(2):
            t = keep.tile([P, T], U8, name=f"x_scales{s}", align_bytes=64)
            x_scales.append(t)
        w1_sc = keep.tile([P, 2 * E, H], U8, name="w1_sc", align_bytes=64)
        w2_sc = keep.tile([P, E, N], U8, name="w2_sc", align_bytes=64)
        ident = keep.tile([P, P], F32, name="ident", align_bytes=64)
        nc.vector.memset(w1_sc[:].rearrange("p a b -> p (a b)").bitcast(I32), 0)
        nc.gpsimd.memset(x_scales[0][:], 0)
        nc.vector.memset(w2_sc[:].rearrange("p a b -> p (a b)").bitcast(I32), 0)
        nc.gpsimd.memset(x_scales[1][:], 0)
        make_identity(nc, ident[:])

        xv = xT.rearrange("(s p j) t -> s p j t", s=2, j=4)
        raw = {}

        def load_x(s):
            for a, b in ((0, 2), (2, 3)):
                r = keep.tile([P, 4, (b - a) * TC], F32, name=f"x_raw{s}_{a}")
                nc.sync.dma_start(out=r[:], in_=xv[s][:, :, a * TC : b * TC])
                for c in range(a, b):
                    raw[s, c] = (r, (c - a) * TC)

        w1_sb = {}

        def load_w1(e):
            w = keep.tile([P, 2, 2 * H], U8, name=f"w1_sb{e}", align_bytes=64)
            nc.sync.dma_start(
                out=w[:].bitcast(I32), in_=w1_words[e].rearrange("s p n -> p s n").bitcast(I32)
            )
            w1_sb[e] = w

        load_x(0)
        nc.sync.dma_start(out=offs_sb[:], in_=offs)
        w1_sv = w1_scales.rearrange("e s (q r) i -> r q (e s) i", r=4)

        def load_w1_scales(a, b):
            for r in range(4):
                nc.sync.dma_start(
                    out=w1_sc[r:P:32, 2 * a : 2 * b].bitcast(I32), in_=w1_sv[r][:, 2 * a : 2 * b].bitcast(I32)
                )

        load_w1_scales(5, 6)
        load_x(1)
        load_w1(5)
        load_w1_scales(0, 5)
        load_w1(4)
        load_w1(3)
        w2_sb = keep.tile([P, E, 2 * N], U8, name="w2_sb", align_bytes=64)
        nc.sync.dma_start(
            out=w2_sb[:].bitcast(I32), in_=w2_words.rearrange("e s p n -> p (e s) n").bitcast(I32)
        )
        w2_sv = w2_scales.rearrange("e s (q r) i -> r q (e s) i", r=4)
        for r in range(4):
            nc.sync.dma_start(out=w2_sc[r:P:32].bitcast(I32), in_=w2_sv[r].bitcast(I32))
        for e in (2, 1, 0):
            load_w1(e)
        gates = []
        for c in range(2):
            g = keep.tile([P, T], F32, name=f"gate{c}")
            gates.append(g)
            nc.sync.dma_start(out=g[:], in_=gate[c])
        nc.sync.dma_start(out=pos1_sb[:], in_=pos1)
        nc.sync.dma_start(out=pos2_sb[:], in_=pos2)

        x_codes = []
        for s in range(2):
            t = keep.tile([P, T], U32, name=f"x_codes{s}", align_bytes=64)
            x_codes.append(t)
        grouped = {}

        def cast_x(s, c, vshare):
            if s == 0:
                g = keep.tile([P, TC, 4], BF16, name=f"x_grouped{s}_{c}", align_bytes=64)
            else:
                g = late.tile([P, TC, 4], BF16, name=f"x_grouped{s}_{c}", tag="late", align_bytes=64)
            r, t0 = raw[s, c]
            src = r[:, :, t0 : t0 + TC].rearrange("p j (c i) -> p c j i", i=4)
            dst = g[:].rearrange("p (c i) j -> p c j i", i=4)
            v = vshare // 4
            if v:
                nc.vector.tensor_copy(out=dst[:, :v], in_=src[:, :v])
            if vshare < TC:
                nc.scalar.copy(out=dst[:, v:], in_=src[:, v:])
            grouped[s, c] = g

        def quantise_x(s, c):
            cols = slice(c * TC, (c + 1) * TC)
            nc.vector.quantize_mx(
                out=x_codes[s][:, cols].bitcast(FP8X4),
                scales=x_scales[s][:, cols],
                in_=grouped[s, c][:].rearrange("p t j -> p (t j)"),
            )

        slot_codes, slot_scales = {}, {}

        def gather(s, t0, t1, what):
            n = (t1 - t0) * P
            ofs = offs_sb[:, t0 * P // 16 : t1 * P // 16]
            pool, tag = (late, "late") if s == 0 and t0 < 8 else (keep, f"slot_{what}{s}_{t0}")
            if what == "w":
                g = pool.tile([P, n], U32, name=f"slot_codes{s}_{t0}", tag=tag, align_bytes=64)
                nc.vector.tensor_copy(out=g[:], in_=x_codes[s][:].indirect(ofs))
                dst = slot_codes
            else:
                g = pool.tile([P, n], U8, name=f"slot_scales{s}_{t0}", tag=tag, align_bytes=64)
                nc.vector.tensor_copy(out=g[:], in_=x_scales[s][:].indirect(ofs))
                dst = slot_scales
            for t in range(t0, t1):
                dst[s, t] = (g, (t - t0) * P)

        acc = {}

        def mm1(t, s):
            e = EXPERT_OF_TILE[t]
            if s == 0:
                a = psum_a.tile([P, H], F32, name="acc")
                acc[t] = a
            g, c0 = slot_codes[s, t]
            z, z0 = slot_scales[s, t]
            nc.tensor.matmul_mx(
                out=acc[t][:],
                lhsT=g[:, c0 : c0 + P].bitcast(FP8X4),
                lhsT_scale=z[:, z0 : z0 + P],
                rhs=w1_sb[e][:, s].bitcast(FP4X4),
                rhs_scale=w1_sc[:, 2 * e + s],
                start=(s == 0),
                stop=(s == 1),
            )

        hid = {}

        def relu(t, engine):
            h = work.tile([P, 2, P, 2], BF16, name="hid", align_bytes=64)
            src = acc[t][:].rearrange("p (r u e) -> p u r e", u=2, e=2)
            if engine == "v":
                nc.vector.tensor_scalar(out=h[:], in0=src, scalar1=0.0, scalar2=None, op0=MAX)
            else:
                nc.scalar.activation(out=h[:], in_=src, func=RELU)
            hid[t] = h

        turned = {}

        def turn(t0, n):
            x = psum_t.tile([P, 2, 2, P], F32, name="turned")
            for j in range(n):
                words = hid[t0 + j][:].rearrange("p u r e -> p (u r e)").bitcast(F32)
                for u in range(2):
                    nc.tensor.transpose(x[:, j, u], words[:, u * P : (u + 1) * P], ident[:])
            turned[t0] = x

        h_grouped = {}

        def ungroup(t0, n, engine):
            g = work.tile([P, 2 * P, 4], BF16, name="h_grouped", align_bytes=64)
            dst = g[:, : n * P].rearrange("p n i -> p (n i)").bitcast(F32).rearrange("p (j n u) -> p j n u", j=n, u=2)
            src = turned[t0][:, :n].rearrange("p j u n -> p j n u")
            if engine == "v":
                nc.vector.tensor_copy(out=dst, in_=src)
            else:
                nc.scalar.copy(out=dst, in_=src)
            h_grouped[t0] = g

        hq = {}

        def quantise_h(t0, n):
            c = work.tile([P, 2 * P], U32, name="h_codes", align_bytes=64)
            z = work.tile([P, 2 * P], U8, name="h_scales", align_bytes=64)
            nc.vector.quantize_mx(
                out=c[:, : n * P].bitcast(FP8X4), scales=z[:, : n * P],
                in_=h_grouped[t0][:, : n * P].rearrange("p n i -> p (n i)"),
            )
            hq[t0] = (c, z)

        y_all = keep.tile([P, S], F32, name="y_all", align_bytes=64)

        def layer2(t0, n, engine):
            c, z = hq[t0]
            y = psum_y.tile([P, 2 * P], F32, name="y")
            if n == 1:
                spans = [(t0, 0, P)]
            elif EXPERT_OF_TILE[t0] == EXPERT_OF_TILE[t0 + 1]:
                spans = [(t0, 0, 2 * P)]
            else:
                spans = [(t0, 0, P), (t0 + 1, P, P)]
            for t, c0, w in spans:
                e = EXPERT_OF_TILE[t]
                nc.tensor.matmul_mx(
                    out=y[:, c0 : c0 + w],
                    lhsT=w2_sb[:, e].bitcast(FP4X4),
                    lhsT_scale=w2_sc[:, e],
                    rhs=c[:, c0 : c0 + w].bitcast(FP8X4),
                    rhs_scale=z[:, c0 : c0 + w],
                    start=True,
                    stop=True,
                )
            dst = y_all[:, t0 * P : (t0 + n) * P]
            if engine == "v":
                nc.vector.tensor_copy(out=dst, in_=y[:, : n * P])
            else:
                nc.scalar.copy(out=dst, in_=y[:, : n * P])

        VS0 = (192, 64, 144)
        for c in range(3):
            cast_x(0, c, VS0[c])
            quantise_x(0, c)
        for c in range(3):
            cast_x(1, c, (96, 128, 160)[c])

        def mm(t):
            mm1(t, 0)
            mm1(t, 1)

        RELUS = "vsssssssssss"
        UNGROUPS = {0: "s", 1: "s", 2: "s", 4: "v", 6: "s", 8: "s", 10: "s"}
        YCOPIES = {0: "v", 1: "s", 2: "s", 4: "v", 6: "v", 8: "s", 10: "s"}

        def chain(t0, n):
            for j in range(n):
                relu(t0 + j, RELUS[t0 + j])
            turn(t0, n)
            ungroup(t0, n, UNGROUPS[t0])
            quantise_h(t0, n)
            layer2(t0, n, YCOPIES[t0])

        gather(0, 8, 12, "w")
        gather(0, 8, 12, "b")
        for t in range(8, 12):
            mm1(t, 0)
        for c in range(3):
            quantise_x(1, c)
        for t0, t1 in ((8, 10), (10, 12)):
            gather(1, t0, t1, "w")
            gather(1, t0, t1, "b")
            for t in range(t0, t1):
                mm1(t, 1)
        gather(0, 4, 8, "w")
        gather(0, 4, 8, "b")
        chain(8, 2)
        gather(1, 6, 8, "w")
        gather(1, 6, 8, "b")
        mm(6)
        mm(7)
        chain(10, 2)
        gather(1, 4, 6, "w")
        gather(1, 4, 6, "b")
        mm(4)
        mm(5)
        chain(6, 2)
        gather(0, 0, 4, "w")
        gather(0, 0, 4, "b")
        chain(4, 2)
        gather(1, 2, 4, "w")
        gather(1, 2, 4, "b")
        mm(2)
        mm(3)
        gather(1, 0, 2, "w")
        gather(1, 1, 2, "b")
        mm(1)
        gather(1, 0, 1, "b")
        mm(0)
        chain(2, 2)
        chain(1, 1)
        chain(0, 1)

        halves = ((0, 512), (512, 768))
        for a, b in halves:
            cols = slice(a // 16, b // 16)
            o1 = keep.tile([P, b - a], F32, name=f"first{a}")
            o2 = keep.tile([P, b - a], F32, name=f"second{a}")
            nc.vector.tensor_tensor(out=o1[:], in0=y_all[:].indirect(pos1_sb[:, cols]), in1=gates[0][:, a:b], op=MULT)
            nc.vector.tensor_tensor(out=o2[:], in0=y_all[:].indirect(pos2_sb[:, cols]), in1=gates[1][:, a:b], op=MULT)
            o = keep.tile([P, b - a], F32, name=f"result{a}")
            nc.vector.tensor_tensor(out=o[:], in0=o1[:], in1=o2[:], op=ADD)
            nc.sync.dma_start(out=out[:, a:b], in_=o[:])
